import numpy as np, ml_dtypes
CORES = [0,1]
N = 2
def setup_inputs(rng):
    return {"x": rng.standard_normal((N, 128, 2048), dtype=np.float32).astype(ml_dtypes.bfloat16)}
def reference(x):
    b = 2048 // N
    blocks = x.reshape(N, 128, N, b)
    return {"y": np.ascontiguousarray(blocks.transpose(2, 1, 0, 3)).reshape(N, 128, 2048)}

SCRATCH = {
    "send": ("sbuf", [128, 1024], "bfloat16"),
    "land": ("sbuf", [128, 1024], "bfloat16"),
}
SEMAPHORES = ["loaded", "sent", "arrived", "stored"]


def rank_program(g, core, T, topo):
    rank = T.rank_of(core)
    if rank is None:
        return

    n = len(T.cores)
    b = T.x.shape[1] // n
    peer_rank = 1 - rank
    peer = T.cores[peer_rank]
    mine = slice(rank * b, (rank + 1) * b)
    theirs = slice(peer_rank * b, (peer_rank + 1) * b)

    g.scalar.dma_start(T.y[:, mine], T.x[:, mine]).then_inc(T.sem.stored, 16)

    g.sync.dma_start(T.send[:], T.x[:, theirs]).then_inc(T.sem.loaded, 16)

    rid, pid, _se = topo.addr(peer)
    engines = topo.mask(core, peer)
    n_eng = bin(engines).count("1")
    g.wait_ge(T.sem.loaded, 16)
    g.remote_dma(T.land[:], T.send[:], T.sem.arrived, T.sem.sent, pid, rid, engines)

    g.sync.wait_ge(T.sem.arrived, n_eng)
    g.sync.dma_start(T.y[:, theirs], T.land[:]).then_inc(T.sem.stored, 16)

    g.wait_ge(T.sem.sent, n_eng)
    g.wait_ge(T.sem.stored, 32)
